import numpy as np
import ml_dtypes


def mxq(x, axis, fmt="e4m3"):
    dtype, down = {"e4m3": (ml_dtypes.float8_e4m3fn, 7), "e5m2": (ml_dtypes.float8_e5m2, 14)}[fmt]
    v = np.moveaxis(np.asarray(x, np.float32).astype(ml_dtypes.bfloat16).astype(np.float64), axis, -1)
    blocks = v.reshape(v.shape[:-1] + (-1, 32))
    amax = np.abs(blocks).max(-1, keepdims=True)
    byte = np.maximum(np.where(amax > 0, np.frexp(amax)[1] - 1 + 127, 0) - down, 1)
    scale = np.exp2(byte - 127.0)
    codes = (blocks / scale).astype(np.float32).astype(dtype).astype(np.float64)
    return np.moveaxis((codes * scale).reshape(v.shape), -1, axis)


WIDE = False


def mx_kscale(k):
    if not WIDE:
        return np.ones(k)
    levels = np.array([10, -10, 5, -5, 0])
    if k % 512:
        return np.exp2(np.random.permutation(np.resize(levels, k // 32))).repeat(32)
    a = np.empty((k // 512, 16))
    for p in range(k // 512):
        a[p, :8] = np.random.permutation(np.resize(levels, 8))
        for g in range(8):
            far = levels[np.abs(levels - a[p, g]) >= 10]
            a[p, g + 8] = far[np.random.randint(len(far))]
    return np.exp2(a.ravel()).repeat(32)


def f64(x):
    return np.asarray(x).astype(np.float64)


def striped(idx):
    return np.tile(np.asarray(idx).reshape(-1, 16).T, (8, 1)).astype(np.uint16)


def unstriped(offs):
    return offs[:16].T.reshape(-1).astype(np.int64)


def striped8(idx):
    return np.asarray(idx).reshape(8, -1, 16).transpose(0, 2, 1).reshape(128, -1).astype(np.uint16)


def unstriped8(offs):
    return offs.reshape(8, 16, -1).transpose(0, 2, 1).reshape(8, -1).astype(np.int64)


def pick8(x, idx, run):
    r = np.arange(len(x))
    return x[r[:, None], idx[r % (8 * run) // run]]


E2M1 = np.array([0.0, 0.5, 1.0, 1.5, 2.0, 3.0, 4.0, 6.0, -0.0, -0.5, -1.0, -1.5, -2.0, -3.0, -4.0, -6.0])


def pack_weight(w, fmt):
    k, n = w.shape
    w = f64(np.asarray(w, np.float32).astype(ml_dtypes.bfloat16)).reshape(k // 32, 32, n)
    amax = np.abs(w).max(1)
    if fmt == "e4m3":
        byte = np.frexp(amax)[1] - 1 + 127 - 7
    else:
        mant, ex = np.frexp(amax / 6.0)
        byte = np.where(mant > 0.5, ex, ex - 1) + 127
    byte = np.clip(np.where(amax > 0, byte, 1), 1, 254)
    scaled = (w * np.exp2(127.0 - byte)[:, None, :]).reshape(k, n).astype(np.float32)
    by_word = np.ascontiguousarray(scaled.reshape(k // 512, 128, 4, n).transpose(0, 1, 3, 2))
    if fmt == "e4m3":
        words = by_word.astype(ml_dtypes.float8_e4m3fn).view(np.uint8)
    else:
        c = by_word.astype(ml_dtypes.float4_e2m1fn).view(np.uint8) & 0xF
        words = (c[..., 0::2] | (c[..., 1::2] << 4)).reshape(k // 512, 128, 2 * n)
    return np.ascontiguousarray(words), np.ascontiguousarray(byte.astype(np.uint8).reshape(k // 512, 16, n))


def unpack_weight(words, scales, fmt):
    g, _, n = scales.shape
    words = np.ascontiguousarray(words).reshape(g, 128, n, -1)
    if fmt == "e4m3":
        vals = words.view(ml_dtypes.float8_e4m3fn).astype(np.float64)
    else:
        nib = np.empty((g, 128, n, 4), np.uint8)
        nib[..., 0::2] = words & 0xF
        nib[..., 1::2] = words >> 4
        vals = E2M1[nib]
    vals = vals * np.repeat(np.exp2(scales.astype(np.float64) - 127.0), 8, axis=1)[..., None]
    return vals.transpose(0, 1, 3, 2).reshape(g * 512, n)


K, J, R, T, U, Z, M, O, C, N, S = 512, 256, 512, 1024, 512, 512, 1024, 128, 512, 256, 1024


def setup_inputs():
    n = np.random.standard_normal
    idx = np.stack([np.random.permutation(T)[:U] for _ in range(8)])
    idx2 = np.random.permutation(U)[:J]
    idx3 = np.random.permutation(M)[:J]
    idx4 = np.stack([np.random.permutation(C)[:J] for _ in range(8)])
    idx5 = np.stack([np.random.permutation(C)[:O] for _ in range(8)])
    idx6 = np.stack([np.random.permutation(J)[:O] for _ in range(8)])
    idx7 = np.random.permutation(S)[:N]
    fk = mx_kscale(K)
    fr = mx_kscale(R)
    fz = mx_kscale(Z)
    wp = pack_weight(n((K, R)) * 1 / np.sqrt(K) / fk[:, None] * fr, "e2m1")
    xop = pack_weight(n((Z, M)) / fz[:, None], "e2m1")
    w2p = pack_weight(n((Z, R)) * 1 / np.sqrt(Z) * fz[:, None] * fr, "e4m3")
    vsp = pack_weight(n((R, S)) * 1 / np.sqrt(R) / fr[:, None], "e4m3")
    return {
        "ta": (np.random.randint(-7, 8, (K, T)).astype(np.float64)).astype(np.float32),
        "ga": ((np.random.randint(8, 25, (K, 1)) / 64.0) * fk[:, None]).astype(np.float32),
        "gb": (np.random.uniform(0.5, 1.6, (K, 1))).astype(np.float32),
        "w_words": wp[0],
        "w_scales": wp[1],
        "xo_words": xop[0],
        "xo_scales": xop[1],
        "w2_words": w2p[0],
        "w2_scales": w2p[1],
        "sa": (np.random.uniform(0.5, 1.6, (R, 1))).astype(np.float32),
        "sb": (np.random.uniform(0.5, 1.6, (R, 1))).astype(np.float32),
        "vs_words": vsp[0],
        "vs_scales": vsp[1],
        "offs": striped8(idx),
        "offs2": striped(idx2),
        "offs3": striped(idx3),
        "offs4": striped8(idx4),
        "offs5": striped8(idx5),
        "offs6": striped8(idx6),
        "offs7": striped(idx7),
    }


def reference(ta, ga, gb, w_words, w_scales, xo_words, xo_scales, w2_words, w2_scales, sa, sb, vs_words, vs_scales, offs, offs2, offs3, offs4, offs5, offs6, offs7):
    idx = unstriped8(offs)
    idx2 = unstriped(offs2)
    idx3 = unstriped(offs3)
    idx4 = unstriped8(offs4)
    idx5 = unstriped8(offs5)
    idx6 = unstriped8(offs6)
    idx7 = unstriped(offs7)
    wu = unpack_weight(w_words, w_scales, "e2m1")
    xou = unpack_weight(xo_words, xo_scales, "e2m1")
    w2u = unpack_weight(w2_words, w2_scales, "e4m3")
    vsu = unpack_weight(vs_words, vs_scales, "e4m3")
    xcd = pick8(f64(ta), idx, 64) * f64(ga)
    xc = xcd[:, idx2] * f64(gb)
    xcq = mxq(xc, 0, "e4m3")
    a = wu.T @ xcq
    xoidx3g = xou[:, idx3]
    b = w2u.T @ xoidx3g
    pw = np.zeros((R, C))
    pw[np.arange(R)[:, None], idx4[np.arange(R) % 512 // 64]] = a
    hid = np.maximum(pick8(pw, idx5, 64) * f64(sa), pick8(b, idx6, 64) * f64(sb))
    vsidx7g = vsu[:, idx7]
    hidq = mxq(hid, 0, "e4m3")
    y = vsidx7g.T @ hidq
    return y

@@ -1,0 +1,210 @@
+from contextlib import ExitStack
+
+import concourse.mybir as mybir
+
+K, J, R, T, U, Z, M, O, C, N, S = 512, 256, 512, 1024, 512, 512, 1024, 128, 512, 256, 1024
+FLOPS = 2 * K * R * J + 2 * Z * R * J + 2 * R * N * O
+
+F32 = mybir.dt.float32
+BF16 = mybir.dt.bfloat16
+I32 = mybir.dt.int32
+U32 = mybir.dt.uint32
+U16 = mybir.dt.uint16
+U8 = mybir.dt.uint8
+FP8X4 = mybir.dt.float8_e4m3fn_x4
+FP4X4 = mybir.dt.float4_e2m1fn_x4
+COPY = mybir.ActivationFunctionType.Copy
+MAX = mybir.AluOpType.max
+
+P = 128
+PACK = 4
+HALF = J // 2
+STRIPE = 16
+VS_ROW = 4
+
+
+def tile_picked_respelled_plain_two_boardmeet_store_plain_kernel(
+    tc, ta, ga, gb, w_words, w_scales, xo_words, xo_scales, w2_words, w2_scales, sa, sb, vs_words, vs_scales,
+    offs, offs2, offs3, offs4, offs5, offs6, offs7, out,
+):
+    nc = tc.nc
+    with ExitStack() as ctx:
+        keep = ctx.enter_context(tc.tile_pool(name="keep", bufs=1))
+        psum = ctx.enter_context(tc.psum_pool(name="psum", bufs=1))
+
+        def load_list(name, src):
+            tile = keep.tile(list(src.shape), U16, name=name)
+            nc.sync.dma_start(tile[:], src)
+            return tile
+
+        def load_column(queue, name, src):
+            tile = keep.tile([P, PACK], F32, name=name)
+            queue.dma_start(tile[:], src.rearrange("(p t) o -> p (t o)", t=PACK))
+            return tile
+
+        def load_words(name, src, dtype, width):
+            tile = keep.tile([P, width], dtype, name=name, align_bytes=64)
+            nc.sync.dma_start(tile[:].bitcast(I32), src.bitcast(I32))
+            return tile
+
+        def load_scale_rows(name, src, first_row, rows):
+            width = src.shape[2] // 4
+            stage = keep.tile([P, 4, width], I32, name=name + "_rows")
+            base = first_row // 32 * 32
+            if rows > 4:
+                nc.vector.memset(stage[base : base + rows], 0)
+            nc.sync.dma_start(stage[first_row : first_row + 4], src[0].bitcast(I32).rearrange("(q i) c -> i q c", i=4))
+            return stage, base, rows
+
+        def spread(name, staged):
+            stage, base, rows = staged
+            plane = keep.tile([P, 4 * stage.shape[2]], U8, name=name, align_bytes=64)
+            if rows < 32:
+                nc.vector.memset(plane[:].bitcast(I32), 0)
+            for q in range(4):
+                nc.vector.tensor_copy(out=plane[32 * q : 32 * q + rows, :].bitcast(I32), in_=stage[base : base + rows, q, :])
+            return plane
+
+        def load_plane(name, src, first_row):
+            plane = keep.tile([P, src.shape[2]], U8, name=name, align_bytes=64)
+            nc.vector.memset(plane[:].bitcast(I32), 0)
+            for q in range(4):
+                rows = slice(32 * q + first_row, 32 * q + first_row + 4)
+                nc.sync.dma_start(plane[rows, :].bitcast(I32), src[0, 4 * q : 4 * q + 4, :].bitcast(I32))
+            return plane
+
+        def load_rows(t):
+            tile = keep.tile([P, T], F32, name="ta%d" % t, tag="ta%d" % t, align_bytes=64)
+            nc.sync.dma_start(tile[:], ta.rearrange("(p t) c -> t p c", t=PACK)[t])
+            return tile
+
+        def dealt(name, src, dtype, copy=nc.vector.tensor_copy, tag=None):
+            tile = keep.tile([P, PACK, P], dtype, name=name, tag=tag or name, align_bytes=64)
+            copy(out=tile[:], in_=src[:].rearrange("p (m t) -> p t m", t=PACK))
+            return tile
+
+        def by_fours(planes):
+            return planes.rearrange("p t (c i) -> p c t i", i=4)
+
+        def woven(tile):
+            return tile.rearrange("p (c i t) -> p c t i", i=4, t=PACK)
+
+        def quantised(name, src, width):
+            codes = keep.tile([P, width], U32, name=name + "_codes", tag=name + "_codes", align_bytes=64)
+            plane = keep.tile([P, width], U8, name=name + "_plane", align_bytes=64)
+            nc.vector.quantize_mx(out=codes[:].bitcast(FP8X4), scales=plane[:], in_=src[:])
+            return codes, plane
+
+        ga_sb = load_column(nc.scalar, "ga_sb", ga)
+        ta_sb = [load_rows(0)]
+        l1 = load_list("l1", offs)
+        ta_sb.append(load_rows(1))
+        ta_sb.append(load_rows(2))
+        l2 = load_list("l2", offs2)
+        w_rows = load_scale_rows("w", w_scales, 0, 4)
+        xo_rows = load_scale_rows("xo", xo_scales, 64, 32)
+        w_raw = load_words("w_raw", w_words[0], U16, R)
+        l3 = load_list("l3", offs3)
+        ta_sb.append(load_rows(3))
+        xo_raw = load_words("xo_raw", xo_words[0], U16, M)
+        l7 = load_list("l7", offs7)
+        vs_plane = load_plane("vs_plane", vs_scales, VS_ROW)
+        w2_plane = load_plane("w2_plane", w2_scales, 0)
+        l4 = load_list("l4", offs4)
+        w2_raw = load_words("w2_raw", w2_words[0].rearrange("p n t -> p (n t)"), U32, R)
+        vs_raw = load_words("vs_raw", vs_words[0].rearrange("p n t -> p (n t)"), U32, S)
+        l6 = load_list("l6", offs6)
+        l5 = load_list("l5", offs5)
+        gb_sb = load_column(nc.gpsimd, "gb_sb", gb)
+        sb_sb = load_column(nc.gpsimd, "sb_sb", sb)
+        sa_sb = load_column(nc.gpsimd, "sa_sb", sa)
+
+        boards = []
+        for t in range(PACK):
+            board = keep.tile([P, C], F32, name="board%d" % t)
+            nc.vector.memset(board[:], 0.0)
+            boards.append(board)
+
+        def respell(planes, xcd, t, h):
+            cols = HALF // STRIPE
+            nc.scalar.activation(out=planes[:, t, :], in_=xcd[:].indirect(l2[:, h * cols : (h + 1) * cols]),
+                                 func=COPY, scale=gb_sb[:, t : t + 1])
+
+        xcd_sb = []
+        planes0 = keep.tile([P, PACK, HALF], BF16, name="planes0", align_bytes=64)
+        for t in range(PACK):
+            xcd = keep.tile([P, U], F32, name="xcd%d" % t)
+            nc.scalar.activation(out=xcd[:], in_=ta_sb[t][:].indirect(l1[:]), func=COPY, scale=ga_sb[:, t : t + 1])
+            xcd_sb.append(xcd)
+        for t in range(PACK):
+            respell(planes0, xcd_sb[t], t, 0)
+
+        w_bytes = dealt("w_bytes", spread("w_plane", w_rows), U8)
+        w_codes = dealt("w_codes", w_raw, U16)
+        xo_bytes = keep.tile([P, J], U8, name="xo_bytes", align_bytes=64)
+        nc.vector.tensor_copy(out=xo_bytes[:], in_=spread("xo_plane", xo_rows)[:].indirect(l3[:]))
+        xo_codes = keep.tile([P, J], U16, name="xo_codes", align_bytes=64)
+        nc.vector.tensor_copy(out=xo_codes[:], in_=xo_raw[:].indirect(l3[:]))
+
+        def first_product(h, planes, groups):
+            xc = keep.tile([P, PACK * HALF], BF16, name="xc%d" % h, tag="xc%d" % h, align_bytes=64)
+            nc.vector.tensor_copy(out=woven(xc[:]), in_=by_fours(planes[:]))
+            codes, plane = quantised("xc%d" % h, xc, HALF)
+            rows = []
+            for g, (tag, ts) in enumerate(groups):
+                bank = psum.tile([P, len(ts), HALF], F32, name="a%d_%d" % (h, g), tag=tag)
+                for i, t in enumerate(ts):
+                    nc.tensor.matmul_mx(out=bank[:, i, :], lhsT=w_codes[:, t, :].bitcast(FP4X4), lhsT_scale=w_bytes[:, t, :],
+                                        rhs=codes[:].bitcast(FP8X4), rhs_scale=plane[:], start=True, stop=True)
+                a_sb = keep.tile([P, len(ts), HALF], F32, name="a_sb%d_%d" % (h, g), tag="a_sb%d_%d" % (h, g), align_bytes=64)
+                nc.scalar.copy(out=a_sb[:], in_=bank[:])
+                rows.extend(a_sb[:, i, :] for i in range(len(ts)))
+            return rows
+
+        def put(rows, h, t):
+            cols = HALF // STRIPE
+            nc.vector.tensor_copy(out=boards[t][:].indirect(l4[:, h * cols : (h + 1) * cols]), in_=rows[t])
+
+        rows0 = first_product(0, planes0, [("bank0", [0]), ("bank1", [1, 2, 3])])
+        vs_bytes = keep.tile([P, N], U8, name="vs_bytes", tag="xc0", align_bytes=64)
+        nc.vector.tensor_copy(out=vs_bytes[:], in_=vs_plane[:].indirect(l7[:]))
+        w2_bytes = dealt("w2_bytes", w2_plane, U8)
+        planes1 = keep.tile([P, PACK, HALF], BF16, name="planes1", tag="ta3", align_bytes=64)
+        for t in range(PACK):
+            respell(planes1, xcd_sb[t], t, 1)
+        rows1 = first_product(1, planes1, [("bank2", [0, 1, 2, 3])])
+        for t in range(PACK):
+            put(rows0, 0, t)
+
+        w2_codes = dealt("w2_codes", w2_raw, U32, nc.scalar.copy, "xc0_codes")
+        second = keep.tile([P, PACK, O], F32, name="second")
+        for g in range(2):
+            bank = psum.tile([P, 2, J], F32, name="b%d" % g, tag="bank%d" % g)
+            for i in range(2):
+                t = 2 * g + i
+                nc.tensor.matmul_mx(out=bank[:, i, :], lhsT=w2_codes[:, t, :].bitcast(FP8X4), lhsT_scale=w2_bytes[:, t, :],
+                                    rhs=xo_codes[:].bitcast(FP4X4), rhs_scale=xo_bytes[:], start=True, stop=True)
+            for i in range(2):
+                t = 2 * g + i
+                b_sb = keep.tile([P, J], F32, name="b_sb%d" % t)
+                nc.scalar.copy(out=b_sb[:], in_=bank[:, i, :])
+                nc.scalar.activation(out=second[:, t, :], in_=b_sb[:].indirect(l6[:]), func=COPY, scale=sb_sb[:, t : t + 1])
+
+        first = keep.tile([P, PACK, O], F32, name="first")
+        for t in range(PACK):
+            put(rows1, 1, t)
+            nc.scalar.activation(out=first[:, t, :], in_=boards[t][:].indirect(l5[:]), func=COPY, scale=sa_sb[:, t : t + 1])
+
+        vs_codes = keep.tile([P, N], U32, name="vs_codes", tag="a_sb1_0", align_bytes=64)
+        nc.vector.tensor_copy(out=vs_codes[:], in_=vs_raw[:].indirect(l7[:]))
+        hid = keep.tile([P, PACK * O], BF16, name="hid", align_bytes=64)
+        nc.vector.tensor_tensor(out=woven(hid[:]), in0=by_fours(first[:]), in1=by_fours(second[:]), op=MAX)
+        hid_codes, hid_plane = quantised("hid", hid, O)
+        for h, (engine, queue) in enumerate(((nc.vector.tensor_copy, nc.sync), (nc.scalar.copy, nc.scalar))):
+            cols = slice(h * P, (h + 1) * P)
+            bank = psum.tile([P, O], F32, name="y%d" % h)
+            nc.tensor.matmul_mx(out=bank[:], lhsT=vs_codes[:, cols].bitcast(FP8X4), lhsT_scale=vs_bytes[VS_ROW:, cols],
+                                rhs=hid_codes[:].bitcast(FP8X4), rhs_scale=hid_plane[:], start=True, stop=True)
+            y_sb = keep.tile([P, O], F32, name="y_sb%d" % h)
+            engine(out=y_sb[:], in_=bank[:])
+            queue.dma_start(out[cols, :], y_sb[:])

@@ -96,6 +96,10 @@ def tile_picked_respelled_plain_two_boardmeet_store_plain_kernel(
             return codes, plane
 
         ga_sb = load_column(nc.scalar, "ga_sb", ga)
+        warm_in = keep.tile([P, 1], F32, name="warm_in")
+        nc.vector.memset(warm_in[:], 0.0)
+        warm_out = keep.tile([P, 1], F32, name="warm_out")
+        nc.scalar.activation(out=warm_out[:], in_=warm_in[:], func=COPY)
         ta_sb = [load_rows(0)]
         l1 = load_list("l1", offs)
         ta_sb.append(load_rows(1))

@@ -17,9 +17,16 @@ COPY = mybir.ActivationFunctionType.Copy
 MAX = mybir.AluOpType.max
 
 P = 128
-PACK = 4
+PARTS = 4
+QUADRANTS = 4
+QUADRANT = P // QUADRANTS
+SCALE_ROWS = 4
+BYTES_A_WORD = 4
 HALF = J // 2
-STRIPE = 16
+HALF_COLUMNS = HALF // 16
+RUN = 4
+ALIGN = 64
+XO_STAGE = 2 * QUADRANT
 VS_ROW = 4
 
 
@@ -37,178 +44,197 @@ def tile_picked_respelled_plain_two_boardmeet_store_plain_kernel(
             nc.sync.dma_start(tile[:], src)
             return tile
 
-        def load_column(queue, name, src):
-            tile = keep.tile([P, PACK], F32, name=name)
-            queue.dma_start(tile[:], src.rearrange("(p t) o -> p (t o)", t=PACK))
+        def load_factors(queue, name, src):
+            tile = keep.tile([P, PARTS], F32, name=name)
+            queue.dma_start(tile[:], src.rearrange("(p t) o -> p (t o)", t=PARTS))
             return tile
 
         def load_words(name, src, dtype, width):
-            tile = keep.tile([P, width], dtype, name=name, align_bytes=64)
+            tile = keep.tile([P, width], dtype, name=name, align_bytes=ALIGN)
             nc.sync.dma_start(tile[:].bitcast(I32), src.bitcast(I32))
             return tile
 
-        def load_scale_rows(name, src, first_row, rows):
-            width = src.shape[2] // 4
-            stage = keep.tile([P, 4, width], I32, name=name + "_rows")
-            base = first_row // 32 * 32
-            if rows > 4:
-                nc.vector.memset(stage[base : base + rows], 0)
-            nc.sync.dma_start(stage[first_row : first_row + 4], src[0].bitcast(I32).rearrange("(q i) c -> i q c", i=4))
-            return stage, base, rows
-
-        def spread(name, staged):
-            stage, base, rows = staged
-            plane = keep.tile([P, 4 * stage.shape[2]], U8, name=name, align_bytes=64)
-            if rows < 32:
-                nc.vector.memset(plane[:].bitcast(I32), 0)
-            for q in range(4):
-                nc.vector.tensor_copy(out=plane[32 * q : 32 * q + rows, :].bitcast(I32), in_=stage[base : base + rows, q, :])
-            return plane
-
-        def load_plane(name, src, first_row):
-            plane = keep.tile([P, src.shape[2]], U8, name=name, align_bytes=64)
-            nc.vector.memset(plane[:].bitcast(I32), 0)
-            for q in range(4):
-                rows = slice(32 * q + first_row, 32 * q + first_row + 4)
-                nc.sync.dma_start(plane[rows, :].bitcast(I32), src[0, 4 * q : 4 * q + 4, :].bitcast(I32))
-            return plane
-
-        def load_rows(t):
-            tile = keep.tile([P, T], F32, name="ta%d" % t, tag="ta%d" % t, align_bytes=64)
-            nc.sync.dma_start(tile[:], ta.rearrange("(p t) c -> t p c", t=PACK)[t])
+        def load_table_part(t):
+            tile = keep.tile([P, T], F32, name="ta%d" % t, tag="ta%d" % t, align_bytes=ALIGN)
+            nc.sync.dma_start(tile[:], ta.rearrange("(p t) c -> t p c", t=PARTS)[t])
             return tile
 
-        def dealt(name, src, dtype, copy=nc.vector.tensor_copy, tag=None):
-            tile = keep.tile([P, PACK, P], dtype, name=name, tag=tag or name, align_bytes=64)
-            copy(out=tile[:], in_=src[:].rearrange("p (m t) -> p t m", t=PACK))
+        def stage_tile(name, src):
+            return keep.tile([P, QUADRANTS, src.shape[2] // BYTES_A_WORD], I32, name=name)
+
+        def load_staged(stage, first, src):
+            rows = src[0].bitcast(I32).rearrange("(q i) c -> i q c", i=SCALE_ROWS)
+            nc.sync.dma_start(stage[first : first + SCALE_ROWS], rows)
+
+        def scale_tile(name, width):
+            return keep.tile([P, width], U8, name=name, align_bytes=ALIGN)
+
+        def clear(tile):
+            nc.vector.memset(tile[:].bitcast(I32), 0)
+
+        def spread(scales, stage, first, rows):
+            for q in range(QUADRANTS):
+                target = scales[QUADRANT * q : QUADRANT * q + rows, :].bitcast(I32)
+                nc.vector.tensor_copy(out=target, in_=stage[first : first + rows, q, :])
+
+        def load_scales(name, src, first):
+            scales = scale_tile(name, src.shape[2])
+            clear(scales)
+            for q in range(QUADRANTS):
+                place = slice(QUADRANT * q + first, QUADRANT * q + first + SCALE_ROWS)
+                rows = src[0, SCALE_ROWS * q : SCALE_ROWS * (q + 1), :]
+                nc.sync.dma_start(scales[place, :].bitcast(I32), rows.bitcast(I32))
+            return scales
+
+        def dealt(name, src, dtype, copy, tag):
+            tile = keep.tile([P, PARTS, P], dtype, name=name, tag=tag, align_bytes=ALIGN)
+            copy(out=tile[:], in_=src[:].rearrange("p (m t) -> p t m", t=PARTS))
             return tile
 
-        def by_fours(planes):
-            return planes.rearrange("p t (c i) -> p c t i", i=4)
+        def gathered(name, window, offsets, dtype, width, tag):
+            tile = keep.tile([P, width], dtype, name=name, tag=tag, align_bytes=ALIGN)
+            nc.vector.tensor_copy(out=tile[:], in_=window[:].indirect(offsets[:]))
+            return tile
 
-        def woven(tile):
-            return tile.rearrange("p (c i t) -> p c t i", i=4, t=PACK)
+        def scaled_gather(target, window, offsets, factors, t):
+            nc.scalar.activation(out=target, in_=window[:].indirect(offsets), func=COPY, scale=factors[:, t : t + 1])
+
+        def by_part(tile):
+            return tile.rearrange("p t (c i) -> p c t i", i=RUN)
+
+        def interleaved(tile):
+            return tile.rearrange("p (c i t) -> p c t i", i=RUN, t=PARTS)
 
         def quantised(name, src, width):
-            codes = keep.tile([P, width], U32, name=name + "_codes", tag=name + "_codes", align_bytes=64)
-            plane = keep.tile([P, width], U8, name=name + "_plane", align_bytes=64)
-            nc.vector.quantize_mx(out=codes[:].bitcast(FP8X4), scales=plane[:], in_=src[:])
-            return codes, plane
+            codes = keep.tile([P, width], U32, name=name + "_codes", tag=name + "_codes", align_bytes=ALIGN)
+            scales = scale_tile(name + "_plane", width)
+            nc.vector.quantize_mx(out=codes[:].bitcast(FP8X4), scales=scales[:], in_=src[:])
+            return codes, scales
 
-        ga_sb = load_column(nc.scalar, "ga_sb", ga)
+        ga_sb = load_factors(nc.scalar, "ga_sb", ga)
         warm_in = keep.tile([P, 1], F32, name="warm_in")
         nc.vector.memset(warm_in[:], 0.0)
         warm_out = keep.tile([P, 1], F32, name="warm_out")
         nc.scalar.activation(out=warm_out[:], in_=warm_in[:], func=COPY)
-        ta_sb = [load_rows(0)]
-        l1 = load_list("l1", offs)
-        ta_sb.append(load_rows(1))
-        ta_sb.append(load_rows(2))
-        l2 = load_list("l2", offs2)
-        w_rows = load_scale_rows("w", w_scales, 0, 4)
-        xo_rows = load_scale_rows("xo", xo_scales, 64, 32)
+        ta_sb = [load_table_part(0)]
+        list1 = load_list("l1", offs)
+        ta_sb.append(load_table_part(1))
+        ta_sb.append(load_table_part(2))
+        list2 = load_list("l2", offs2)
+        w_stage = stage_tile("w_rows", w_scales)
+        load_staged(w_stage, 0, w_scales)
+        xo_stage = stage_tile("xo_rows", xo_scales)
+        nc.vector.memset(xo_stage[XO_STAGE : XO_STAGE + QUADRANT], 0)
+        load_staged(xo_stage, XO_STAGE, xo_scales)
         w_raw = load_words("w_raw", w_words[0], U16, R)
-        l3 = load_list("l3", offs3)
-        ta_sb.append(load_rows(3))
+        list3 = load_list("l3", offs3)
+        ta_sb.append(load_table_part(3))
         xo_raw = load_words("xo_raw", xo_words[0], U16, M)
-        l7 = load_list("l7", offs7)
-        vs_plane = load_plane("vs_plane", vs_scales, VS_ROW)
-        w2_plane = load_plane("w2_plane", w2_scales, 0)
-        l4 = load_list("l4", offs4)
+        list7 = load_list("l7", offs7)
+        vs_scales_sb = load_scales("vs_plane", vs_scales, VS_ROW)
+        w2_scales_sb = load_scales("w2_plane", w2_scales, 0)
+        list4 = load_list("l4", offs4)
         w2_raw = load_words("w2_raw", w2_words[0].rearrange("p n t -> p (n t)"), U32, R)
         vs_raw = load_words("vs_raw", vs_words[0].rearrange("p n t -> p (n t)"), U32, S)
-        l6 = load_list("l6", offs6)
-        l5 = load_list("l5", offs5)
-        gb_sb = load_column(nc.gpsimd, "gb_sb", gb)
-        sb_sb = load_column(nc.gpsimd, "sb_sb", sb)
-        sa_sb = load_column(nc.gpsimd, "sa_sb", sa)
+        list6 = load_list("l6", offs6)
+        list5 = load_list("l5", offs5)
+        gb_sb = load_factors(nc.gpsimd, "gb_sb", gb)
+        sb_sb = load_factors(nc.gpsimd, "sb_sb", sb)
+        sa_sb = load_factors(nc.gpsimd, "sa_sb", sa)
 
         boards = []
-        for t in range(PACK):
+        for t in range(PARTS):
             board = keep.tile([P, C], F32, name="board%d" % t)
             nc.vector.memset(board[:], 0.0)
             boards.append(board)
 
-        def respell(planes, xcd, t, h):
-            cols = HALF // STRIPE
-            nc.scalar.activation(out=planes[:, t, :], in_=xcd[:].indirect(l2[:, h * cols : (h + 1) * cols]),
-                                 func=COPY, scale=gb_sb[:, t : t + 1])
+        def half_of(offsets, h):
+            return offsets[:, h * HALF_COLUMNS : (h + 1) * HALF_COLUMNS]
 
         xcd_sb = []
-        planes0 = keep.tile([P, PACK, HALF], BF16, name="planes0", align_bytes=64)
-        for t in range(PACK):
+        xc_parts0 = keep.tile([P, PARTS, HALF], BF16, name="planes0", align_bytes=ALIGN)
+        for t in range(PARTS):
             xcd = keep.tile([P, U], F32, name="xcd%d" % t)
-            nc.scalar.activation(out=xcd[:], in_=ta_sb[t][:].indirect(l1[:]), func=COPY, scale=ga_sb[:, t : t + 1])
+            scaled_gather(xcd[:], ta_sb[t], list1[:], ga_sb, t)
             xcd_sb.append(xcd)
-        for t in range(PACK):
-            respell(planes0, xcd_sb[t], t, 0)
+        for t in range(PARTS):
+            scaled_gather(xc_parts0[:, t, :], xcd_sb[t], half_of(list2, 0), gb_sb, t)
 
-        w_bytes = dealt("w_bytes", spread("w_plane", w_rows), U8)
-        w_codes = dealt("w_codes", w_raw, U16)
-        xo_bytes = keep.tile([P, J], U8, name="xo_bytes", align_bytes=64)
-        nc.vector.tensor_copy(out=xo_bytes[:], in_=spread("xo_plane", xo_rows)[:].indirect(l3[:]))
-        xo_codes = keep.tile([P, J], U16, name="xo_codes", align_bytes=64)
-        nc.vector.tensor_copy(out=xo_codes[:], in_=xo_raw[:].indirect(l3[:]))
+        w_scales_sb = scale_tile("w_plane", R)
+        clear(w_scales_sb)
+        spread(w_scales_sb, w_stage, 0, SCALE_ROWS)
+        w_bytes = dealt("w_bytes", w_scales_sb, U8, nc.vector.tensor_copy, "w_bytes")
+        w_codes = dealt("w_codes", w_raw, U16, nc.vector.tensor_copy, "w_codes")
+        xo_bytes = scale_tile("xo_bytes", J)
+        xo_scales_sb = scale_tile("xo_plane", M)
+        spread(xo_scales_sb, xo_stage, XO_STAGE, QUADRANT)
+        nc.vector.tensor_copy(out=xo_bytes[:], in_=xo_scales_sb[:].indirect(list3[:]))
+        xo_codes = gathered("xo_codes", xo_raw, list3, U16, J, "xo_codes")
 
-        def first_product(h, planes, groups):
-            xc = keep.tile([P, PACK * HALF], BF16, name="xc%d" % h, tag="xc%d" % h, align_bytes=64)
-            nc.vector.tensor_copy(out=woven(xc[:]), in_=by_fours(planes[:]))
-            codes, plane = quantised("xc%d" % h, xc, HALF)
-            rows = []
-            for g, (tag, ts) in enumerate(groups):
-                bank = psum.tile([P, len(ts), HALF], F32, name="a%d_%d" % (h, g), tag=tag)
-                for i, t in enumerate(ts):
-                    nc.tensor.matmul_mx(out=bank[:, i, :], lhsT=w_codes[:, t, :].bitcast(FP4X4), lhsT_scale=w_bytes[:, t, :],
-                                        rhs=codes[:].bitcast(FP8X4), rhs_scale=plane[:], start=True, stop=True)
-                a_sb = keep.tile([P, len(ts), HALF], F32, name="a_sb%d_%d" % (h, g), tag="a_sb%d_%d" % (h, g), align_bytes=64)
+        def first_product(h, xc_parts, banks):
+            xc = keep.tile([P, PARTS * HALF], BF16, name="xc%d" % h, tag="xc%d" % h, align_bytes=ALIGN)
+            nc.vector.tensor_copy(out=interleaved(xc[:]), in_=by_part(xc_parts[:]))
+            codes, scales = quantised("xc%d" % h, xc, HALF)
+            a_parts = []
+            for g, (tag, parts) in enumerate(banks):
+                bank = psum.tile([P, len(parts), HALF], F32, name="a%d_%d" % (h, g), tag=tag)
+                for i, t in enumerate(parts):
+                    nc.tensor.matmul_mx(
+                        out=bank[:, i, :], lhsT=w_codes[:, t, :].bitcast(FP4X4), lhsT_scale=w_bytes[:, t, :],
+                        rhs=codes[:].bitcast(FP8X4), rhs_scale=scales[:], start=True, stop=True,
+                    )
+                name = "a_sb%d_%d" % (h, g)
+                a_sb = keep.tile([P, len(parts), HALF], F32, name=name, tag=name, align_bytes=ALIGN)
                 nc.scalar.copy(out=a_sb[:], in_=bank[:])
-                rows.extend(a_sb[:, i, :] for i in range(len(ts)))
-            return rows
+                a_parts.extend(a_sb[:, i, :] for i in range(len(parts)))
+            return a_parts
 
-        def put(rows, h, t):
-            cols = HALF // STRIPE
-            nc.vector.tensor_copy(out=boards[t][:].indirect(l4[:, h * cols : (h + 1) * cols]), in_=rows[t])
+        def put_on_board(a_parts, h, t):
+            nc.vector.tensor_copy(out=boards[t][:].indirect(half_of(list4, h)), in_=a_parts[t])
 
-        rows0 = first_product(0, planes0, [("bank0", [0]), ("bank1", [1, 2, 3])])
-        vs_bytes = keep.tile([P, N], U8, name="vs_bytes", tag="xc0", align_bytes=64)
-        nc.vector.tensor_copy(out=vs_bytes[:], in_=vs_plane[:].indirect(l7[:]))
-        w2_bytes = dealt("w2_bytes", w2_plane, U8)
-        planes1 = keep.tile([P, PACK, HALF], BF16, name="planes1", tag="ta3", align_bytes=64)
-        for t in range(PACK):
-            respell(planes1, xcd_sb[t], t, 1)
-        rows1 = first_product(1, planes1, [("bank2", [0, 1, 2, 3])])
-        for t in range(PACK):
-            put(rows0, 0, t)
+        a_half0 = first_product(0, xc_parts0, [("bank0", [0]), ("bank1", [1, 2, 3])])
+        vs_bytes = gathered("vs_bytes", vs_scales_sb, list7, U8, N, "xc0")
+        w2_bytes = dealt("w2_bytes", w2_scales_sb, U8, nc.vector.tensor_copy, "w2_bytes")
+        xc_parts1 = keep.tile([P, PARTS, HALF], BF16, name="planes1", tag="ta3", align_bytes=ALIGN)
+        for t in range(PARTS):
+            scaled_gather(xc_parts1[:, t, :], xcd_sb[t], half_of(list2, 1), gb_sb, t)
+        a_half1 = first_product(1, xc_parts1, [("bank2", [0, 1, 2, 3])])
+        for t in range(PARTS):
+            put_on_board(a_half0, 0, t)
 
         w2_codes = dealt("w2_codes", w2_raw, U32, nc.scalar.copy, "xc0_codes")
-        second = keep.tile([P, PACK, O], F32, name="second")
-        for g in range(2):
-            bank = psum.tile([P, 2, J], F32, name="b%d" % g, tag="bank%d" % g)
-            for i in range(2):
-                t = 2 * g + i
-                nc.tensor.matmul_mx(out=bank[:, i, :], lhsT=w2_codes[:, t, :].bitcast(FP8X4), lhsT_scale=w2_bytes[:, t, :],
-                                    rhs=xo_codes[:].bitcast(FP4X4), rhs_scale=xo_bytes[:], start=True, stop=True)
-            for i in range(2):
-                t = 2 * g + i
+        from_b = keep.tile([P, PARTS, O], F32, name="second")
+        in_bank = 2
+        for g in range(PARTS // in_bank):
+            bank = psum.tile([P, in_bank, J], F32, name="b%d" % g, tag="bank%d" % g)
+            for i in range(in_bank):
+                t = in_bank * g + i
+                nc.tensor.matmul_mx(
+                    out=bank[:, i, :], lhsT=w2_codes[:, t, :].bitcast(FP8X4), lhsT_scale=w2_bytes[:, t, :],
+                    rhs=xo_codes[:].bitcast(FP4X4), rhs_scale=xo_bytes[:], start=True, stop=True,
+                )
+            for i in range(in_bank):
+                t = in_bank * g + i
                 b_sb = keep.tile([P, J], F32, name="b_sb%d" % t)
                 nc.scalar.copy(out=b_sb[:], in_=bank[:, i, :])
-                nc.scalar.activation(out=second[:, t, :], in_=b_sb[:].indirect(l6[:]), func=COPY, scale=sb_sb[:, t : t + 1])
+                scaled_gather(from_b[:, t, :], b_sb, list6[:], sb_sb, t)
 
-        first = keep.tile([P, PACK, O], F32, name="first")
-        for t in range(PACK):
-            put(rows1, 1, t)
-            nc.scalar.activation(out=first[:, t, :], in_=boards[t][:].indirect(l5[:]), func=COPY, scale=sa_sb[:, t : t + 1])
+        from_board = keep.tile([P, PARTS, O], F32, name="first")
+        for t in range(PARTS):
+            put_on_board(a_half1, 1, t)
+            scaled_gather(from_board[:, t, :], boards[t], list5[:], sa_sb, t)
 
-        vs_codes = keep.tile([P, N], U32, name="vs_codes", tag="a_sb1_0", align_bytes=64)
-        nc.vector.tensor_copy(out=vs_codes[:], in_=vs_raw[:].indirect(l7[:]))
-        hid = keep.tile([P, PACK * O], BF16, name="hid", align_bytes=64)
-        nc.vector.tensor_tensor(out=woven(hid[:]), in0=by_fours(first[:]), in1=by_fours(second[:]), op=MAX)
-        hid_codes, hid_plane = quantised("hid", hid, O)
-        for h, (engine, queue) in enumerate(((nc.vector.tensor_copy, nc.sync), (nc.scalar.copy, nc.scalar))):
-            cols = slice(h * P, (h + 1) * P)
-            bank = psum.tile([P, O], F32, name="y%d" % h)
-            nc.tensor.matmul_mx(out=bank[:], lhsT=vs_codes[:, cols].bitcast(FP8X4), lhsT_scale=vs_bytes[VS_ROW:, cols],
-                                rhs=hid_codes[:].bitcast(FP8X4), rhs_scale=hid_plane[:], start=True, stop=True)
-            y_sb = keep.tile([P, O], F32, name="y_sb%d" % h)
-            engine(out=y_sb[:], in_=bank[:])
-            queue.dma_start(out[cols, :], y_sb[:])
+        vs_codes = gathered("vs_codes", vs_raw, list7, U32, N, "a_sb1_0")
+        hid = keep.tile([P, PARTS * O], BF16, name="hid", align_bytes=ALIGN)
+        nc.vector.tensor_tensor(out=interleaved(hid[:]), in0=by_part(from_board[:]), in1=by_part(from_b[:]), op=MAX)
+        hid_codes, hid_scales = quantised("hid", hid, O)
+        for block, (copy, queue) in enumerate(((nc.vector.tensor_copy, nc.sync), (nc.scalar.copy, nc.scalar))):
+            rows = slice(block * P, (block + 1) * P)
+            bank = psum.tile([P, O], F32, name="y%d" % block)
+            nc.tensor.matmul_mx(
+                out=bank[:], lhsT=vs_codes[:, rows].bitcast(FP8X4), lhsT_scale=vs_bytes[VS_ROW:, rows],
+                rhs=hid_codes[:].bitcast(FP8X4), rhs_scale=hid_scales[:], start=True, stop=True,
+            )
+            y_sb = keep.tile([P, O], F32, name="y_sb%d" % block)
+            copy(out=y_sb[:], in_=bank[:])
+            queue.dma_start(out[rows, :], y_sb[:])

from contextlib import ExitStack

import concourse.mybir as mybir

K, J, R, T, U, Z, M, O, C, N, S = 512, 256, 512, 1024, 512, 512, 1024, 128, 512, 256, 1024
FLOPS = 2 * K * R * J + 2 * Z * R * J + 2 * R * N * O

F32 = mybir.dt.float32
BF16 = mybir.dt.bfloat16
I32 = mybir.dt.int32
U32 = mybir.dt.uint32
U16 = mybir.dt.uint16
U8 = mybir.dt.uint8
FP8X4 = mybir.dt.float8_e4m3fn_x4
FP4X4 = mybir.dt.float4_e2m1fn_x4
COPY = mybir.ActivationFunctionType.Copy
MAX = mybir.AluOpType.max

P = 128
PARTS = 4
QUADRANTS = 4
QUADRANT = P // QUADRANTS
SCALE_ROWS = 4
BYTES_A_WORD = 4
HALF = J // 2
HALF_COLUMNS = HALF // 16
RUN = 4
ALIGN = 64
XO_STAGE = 2 * QUADRANT
VS_ROW = 4


def tile_picked_respelled_plain_two_boardmeet_store_plain_kernel(
    tc, ta, ga, gb, w_words, w_scales, xo_words, xo_scales, w2_words, w2_scales, sa, sb, vs_words, vs_scales,
    offs, offs2, offs3, offs4, offs5, offs6, offs7, out,
):
    nc = tc.nc
    with ExitStack() as ctx:
        keep = ctx.enter_context(tc.tile_pool(name="keep", bufs=1))
        psum = ctx.enter_context(tc.psum_pool(name="psum", bufs=1))

        def load_list(name, src):
            tile = keep.tile(list(src.shape), U16, name=name)
            nc.sync.dma_start(tile[:], src)
            return tile

        def load_factors(queue, name, src):
            tile = keep.tile([P, PARTS], F32, name=name)
            queue.dma_start(tile[:], src.rearrange("(p t) o -> p (t o)", t=PARTS))
            return tile

        def load_words(name, src, dtype, width):
            tile = keep.tile([P, width], dtype, name=name, align_bytes=ALIGN)
            nc.sync.dma_start(tile[:].bitcast(I32), src.bitcast(I32))
            return tile

        def load_table_part(t):
            tile = keep.tile([P, T], F32, name="ta%d" % t, tag="ta%d" % t, align_bytes=ALIGN)
            nc.sync.dma_start(tile[:], ta.rearrange("(p t) c -> t p c", t=PARTS)[t])
            return tile

        def stage_tile(name, src):
            return keep.tile([P, QUADRANTS, src.shape[2] // BYTES_A_WORD], I32, name=name)

        def load_staged(stage, first, src):
            rows = src[0].bitcast(I32).rearrange("(q i) c -> i q c", i=SCALE_ROWS)
            nc.sync.dma_start(stage[first : first + SCALE_ROWS], rows)

        def scale_tile(name, width):
            return keep.tile([P, width], U8, name=name, align_bytes=ALIGN)

        def clear(tile):
            nc.vector.memset(tile[:].bitcast(I32), 0)

        def spread(scales, stage, first, rows):
            for q in range(QUADRANTS):
                target = scales[QUADRANT * q : QUADRANT * q + rows, :].bitcast(I32)
                nc.vector.tensor_copy(out=target, in_=stage[first : first + rows, q, :])

        def load_scales(name, src, first):
            scales = scale_tile(name, src.shape[2])
            clear(scales)
            for q in range(QUADRANTS):
                place = slice(QUADRANT * q + first, QUADRANT * q + first + SCALE_ROWS)
                rows = src[0, SCALE_ROWS * q : SCALE_ROWS * (q + 1), :]
                nc.sync.dma_start(scales[place, :].bitcast(I32), rows.bitcast(I32))
            return scales

        def dealt(name, src, dtype, copy, tag):
            tile = keep.tile([P, PARTS, P], dtype, name=name, tag=tag, align_bytes=ALIGN)
            copy(out=tile[:], in_=src[:].rearrange("p (m t) -> p t m", t=PARTS))
            return tile

        def gathered(name, window, offsets, dtype, width, tag):
            tile = keep.tile([P, width], dtype, name=name, tag=tag, align_bytes=ALIGN)
            nc.vector.tensor_copy(out=tile[:], in_=window[:].indirect(offsets[:]))
            return tile

        def scaled_gather(target, window, offsets, factors, t):
            nc.scalar.activation(out=target, in_=window[:].indirect(offsets), func=COPY, scale=factors[:, t : t + 1])

        def by_part(tile):
            return tile.rearrange("p t (c i) -> p c t i", i=RUN)

        def interleaved(tile):
            return tile.rearrange("p (c i t) -> p c t i", i=RUN, t=PARTS)

        def quantised(name, src, width):
            codes = keep.tile([P, width], U32, name=name + "_codes", tag=name + "_codes", align_bytes=ALIGN)
            scales = scale_tile(name + "_plane", width)
            nc.vector.quantize_mx(out=codes[:].bitcast(FP8X4), scales=scales[:], in_=src[:])
            return codes, scales

        ga_sb = load_factors(nc.scalar, "ga_sb", ga)
        warm_in = keep.tile([P, 1], F32, name="warm_in")
        nc.vector.memset(warm_in[:], 0.0)
        warm_out = keep.tile([P, 1], F32, name="warm_out")
        nc.scalar.activation(out=warm_out[:], in_=warm_in[:], func=COPY)
        ta_sb = [load_table_part(0)]
        list1 = load_list("l1", offs)
        ta_sb.append(load_table_part(1))
        ta_sb.append(load_table_part(2))
        list2 = load_list("l2", offs2)
        w_stage = stage_tile("w_rows", w_scales)
        load_staged(w_stage, 0, w_scales)
        xo_stage = stage_tile("xo_rows", xo_scales)
        nc.vector.memset(xo_stage[XO_STAGE : XO_STAGE + QUADRANT], 0)
        load_staged(xo_stage, XO_STAGE, xo_scales)
        w_raw = load_words("w_raw", w_words[0], U16, R)
        list3 = load_list("l3", offs3)
        ta_sb.append(load_table_part(3))
        xo_raw = load_words("xo_raw", xo_words[0], U16, M)
        list7 = load_list("l7", offs7)
        vs_scales_sb = load_scales("vs_plane", vs_scales, VS_ROW)
        w2_scales_sb = load_scales("w2_plane", w2_scales, 0)
        list4 = load_list("l4", offs4)
        w2_raw = load_words("w2_raw", w2_words[0].rearrange("p n t -> p (n t)"), U32, R)
        vs_raw = load_words("vs_raw", vs_words[0].rearrange("p n t -> p (n t)"), U32, S)
        list6 = load_list("l6", offs6)
        list5 = load_list("l5", offs5)
        gb_sb = load_factors(nc.gpsimd, "gb_sb", gb)
        sb_sb = load_factors(nc.gpsimd, "sb_sb", sb)
        sa_sb = load_factors(nc.gpsimd, "sa_sb", sa)

        boards = []
        for t in range(PARTS):
            board = keep.tile([P, C], F32, name="board%d" % t)
            nc.vector.memset(board[:], 0.0)
            boards.append(board)

        def half_of(offsets, h):
            return offsets[:, h * HALF_COLUMNS : (h + 1) * HALF_COLUMNS]

        xcd_sb = []
        xc_parts0 = keep.tile([P, PARTS, HALF], BF16, name="planes0", align_bytes=ALIGN)
        for t in range(PARTS):
            xcd = keep.tile([P, U], F32, name="xcd%d" % t)
            scaled_gather(xcd[:], ta_sb[t], list1[:], ga_sb, t)
            xcd_sb.append(xcd)
        for t in range(PARTS):
            scaled_gather(xc_parts0[:, t, :], xcd_sb[t], half_of(list2, 0), gb_sb, t)

        w_scales_sb = scale_tile("w_plane", R)
        clear(w_scales_sb)
        spread(w_scales_sb, w_stage, 0, SCALE_ROWS)
        w_bytes = dealt("w_bytes", w_scales_sb, U8, nc.vector.tensor_copy, "w_bytes")
        w_codes = dealt("w_codes", w_raw, U16, nc.vector.tensor_copy, "w_codes")
        xo_bytes = scale_tile("xo_bytes", J)
        xo_scales_sb = scale_tile("xo_plane", M)
        spread(xo_scales_sb, xo_stage, XO_STAGE, QUADRANT)
        nc.vector.tensor_copy(out=xo_bytes[:], in_=xo_scales_sb[:].indirect(list3[:]))
        xo_codes = gathered("xo_codes", xo_raw, list3, U16, J, "xo_codes")

        def first_product(h, xc_parts, banks):
            xc = keep.tile([P, PARTS * HALF], BF16, name="xc%d" % h, tag="xc%d" % h, align_bytes=ALIGN)
            nc.vector.tensor_copy(out=interleaved(xc[:]), in_=by_part(xc_parts[:]))
            codes, scales = quantised("xc%d" % h, xc, HALF)
            a_parts = []
            for g, (tag, parts) in enumerate(banks):
                bank = psum.tile([P, len(parts), HALF], F32, name="a%d_%d" % (h, g), tag=tag)
                for i, t in enumerate(parts):
                    nc.tensor.matmul_mx(
                        out=bank[:, i, :], lhsT=w_codes[:, t, :].bitcast(FP4X4), lhsT_scale=w_bytes[:, t, :],
                        rhs=codes[:].bitcast(FP8X4), rhs_scale=scales[:], start=True, stop=True,
                    )
                name = "a_sb%d_%d" % (h, g)
                a_sb = keep.tile([P, len(parts), HALF], F32, name=name, tag=name, align_bytes=ALIGN)
                nc.scalar.copy(out=a_sb[:], in_=bank[:])
                a_parts.extend(a_sb[:, i, :] for i in range(len(parts)))
            return a_parts

        def put_on_board(a_parts, h, t):
            nc.vector.tensor_copy(out=boards[t][:].indirect(half_of(list4, h)), in_=a_parts[t])

        a_half0 = first_product(0, xc_parts0, [("bank0", [0]), ("bank1", [1, 2, 3])])
        vs_bytes = gathered("vs_bytes", vs_scales_sb, list7, U8, N, "xc0")
        w2_bytes = dealt("w2_bytes", w2_scales_sb, U8, nc.vector.tensor_copy, "w2_bytes")
        xc_parts1 = keep.tile([P, PARTS, HALF], BF16, name="planes1", tag="ta3", align_bytes=ALIGN)
        for t in range(PARTS):
            scaled_gather(xc_parts1[:, t, :], xcd_sb[t], half_of(list2, 1), gb_sb, t)
        a_half1 = first_product(1, xc_parts1, [("bank2", [0, 1, 2, 3])])
        for t in range(PARTS):
            put_on_board(a_half0, 0, t)

        w2_codes = dealt("w2_codes", w2_raw, U32, nc.scalar.copy, "xc0_codes")
        from_b = keep.tile([P, PARTS, O], F32, name="second")
        in_bank = 2
        for g in range(PARTS // in_bank):
            bank = psum.tile([P, in_bank, J], F32, name="b%d" % g, tag="bank%d" % g)
            for i in range(in_bank):
                t = in_bank * g + i
                nc.tensor.matmul_mx(
                    out=bank[:, i, :], lhsT=w2_codes[:, t, :].bitcast(FP8X4), lhsT_scale=w2_bytes[:, t, :],
                    rhs=xo_codes[:].bitcast(FP4X4), rhs_scale=xo_bytes[:], start=True, stop=True,
                )
            for i in range(in_bank):
                t = in_bank * g + i
                b_sb = keep.tile([P, J], F32, name="b_sb%d" % t)
                nc.scalar.copy(out=b_sb[:], in_=bank[:, i, :])
                scaled_gather(from_b[:, t, :], b_sb, list6[:], sb_sb, t)

        from_board = keep.tile([P, PARTS, O], F32, name="first")
        for t in range(PARTS):
            put_on_board(a_half1, 1, t)
            scaled_gather(from_board[:, t, :], boards[t], list5[:], sa_sb, t)

        vs_codes = gathered("vs_codes", vs_raw, list7, U32, N, "a_sb1_0")
        hid = keep.tile([P, PARTS * O], BF16, name="hid", align_bytes=ALIGN)
        nc.vector.tensor_tensor(out=interleaved(hid[:]), in0=by_part(from_board[:]), in1=by_part(from_b[:]), op=MAX)
        hid_codes, hid_scales = quantised("hid", hid, O)
        for block, (copy, queue) in enumerate(((nc.vector.tensor_copy, nc.sync), (nc.scalar.copy, nc.scalar))):
            rows = slice(block * P, (block + 1) * P)
            bank = psum.tile([P, O], F32, name="y%d" % block)
            nc.tensor.matmul_mx(
                out=bank[:], lhsT=vs_codes[:, rows].bitcast(FP8X4), lhsT_scale=vs_bytes[VS_ROW:, rows],
                rhs=hid_codes[:].bitcast(FP8X4), rhs_scale=hid_scales[:], start=True, stop=True,
            )
            y_sb = keep.tile([P, O], F32, name="y_sb%d" % block)
            copy(out=y_sb[:], in_=bank[:])
            queue.dma_start(out[rows, :], y_sb[:])
